import numpy as np
import ml_dtypes


def mxq(x, axis, fmt="e4m3"):
    dtype, down = {"e4m3": (ml_dtypes.float8_e4m3fn, 7), "e5m2": (ml_dtypes.float8_e5m2, 14)}[fmt]
    v = np.moveaxis(np.asarray(x, np.float32).astype(ml_dtypes.bfloat16).astype(np.float64), axis, -1)
    blocks = v.reshape(v.shape[:-1] + (-1, 32))
    amax = np.abs(blocks).max(-1, keepdims=True)
    byte = np.maximum(np.where(amax > 0, np.frexp(amax)[1] - 1 + 127, 0) - down, 1)
    scale = np.exp2(byte - 127.0)
    codes = (blocks / scale).astype(np.float32).astype(dtype).astype(np.float64)
    return np.moveaxis((codes * scale).reshape(v.shape), -1, axis)


WIDE = False


def mx_kscale(k):
    if not WIDE:
        return np.ones(k)
    levels = np.array([10, -10, 5, -5, 0])
    if k % 512:
        return np.exp2(np.random.permutation(np.resize(levels, k // 32))).repeat(32)
    a = np.empty((k // 512, 16))
    for p in range(k // 512):
        a[p, :8] = np.random.permutation(np.resize(levels, 8))
        for g in range(8):
            far = levels[np.abs(levels - a[p, g]) >= 10]
            a[p, g + 8] = far[np.random.randint(len(far))]
    return np.exp2(a.ravel()).repeat(32)


def f64(x):
    return np.asarray(x).astype(np.float64)


def striped(idx):
    return np.tile(idx.reshape(-1, 16).T, (8, 1)).astype(np.uint16)


def unstriped(offs):
    return offs[:16].T.reshape(-1).astype(np.int64)


E2M1 = np.array([0.0, 0.5, 1.0, 1.5, 2.0, 3.0, 4.0, 6.0, -0.0, -0.5, -1.0, -1.5, -2.0, -3.0, -4.0, -6.0])


def pack_weight(w, fmt):
    k, n = w.shape
    w = f64(np.asarray(w, np.float32).astype(ml_dtypes.bfloat16)).reshape(k // 32, 32, n)
    amax = np.abs(w).max(1)
    if fmt == "e4m3":
        byte = np.frexp(amax)[1] - 1 + 127 - 7
    else:
        mant, ex = np.frexp(amax / 6.0)
        byte = np.where(mant > 0.5, ex, ex - 1) + 127
    byte = np.clip(np.where(amax > 0, byte, 1), 1, 254)
    scaled = (w * np.exp2(127.0 - byte)[:, None, :]).reshape(k, n).astype(np.float32)
    by_word = np.ascontiguousarray(scaled.reshape(k // 512, 128, 4, n).transpose(0, 1, 3, 2))
    if fmt == "e4m3":
        words = by_word.astype(ml_dtypes.float8_e4m3fn).view(np.uint8)
    else:
        c = by_word.astype(ml_dtypes.float4_e2m1fn).view(np.uint8) & 0xF
        words = (c[..., 0::2] | (c[..., 1::2] << 4)).reshape(k // 512, 128, 2 * n)
    return np.ascontiguousarray(words), np.ascontiguousarray(byte.astype(np.uint8).reshape(k // 512, 16, n))


def unpack_weight(words, scales, fmt):
    g, _, n = scales.shape
    words = np.ascontiguousarray(words).reshape(g, 128, n, -1)
    if fmt == "e4m3":
        vals = words.view(ml_dtypes.float8_e4m3fn).astype(np.float64)
    else:
        nib = np.empty((g, 128, n, 4), np.uint8)
        nib[..., 0::2] = words & 0xF
        nib[..., 1::2] = words >> 4
        vals = E2M1[nib]
    vals = vals * np.repeat(np.exp2(scales.astype(np.float64) - 127.0), 8, axis=1)[..., None]
    return vals.transpose(0, 1, 3, 2).reshape(g * 512, n)


def gelu(v):
    return 0.5 * v * (1.0 + np.tanh(np.sqrt(2.0 / np.pi) * (v + 0.044715 * v**3)))


K, H, T, S, P = 1536, 1024, 2048, 1024, 512

def setup_inputs():
    n = np.random.standard_normal
    s = mx_kscale(K)[:, None]
    u = mx_kscale(H)[:, None]
    tab_words, tab_scales = pack_weight(n((K, T)) * s, "e4m3")
    w1 = 1.5 * n((K, H)) / np.sqrt(K) / s
    w4_words, w4_scales = pack_weight(n((H, P)) / np.sqrt(H) / u, "e2m1")
    gain = np.exp(0.3 * n(H)) * u[:, 0]
    prof = 0.5 * n(H) * u[:, 0]
    ew = n(H) / np.sqrt(H) / u[:, 0] ** 2
    jw = np.exp(0.4 * n(P))
    return {
        "tab_words": tab_words, "tab_scales": tab_scales,
        "offs": striped(np.random.permutation(T)[:S]),
        "pos1": striped(np.random.permutation(S)[:P]),
        "pos2": striped(np.random.permutation(S)[:P]),
        "w1": w1.astype(np.float32),
        "w4_words": w4_words, "w4_scales": w4_scales,
        "gain": gain.astype(np.float32), "prof": prof.astype(np.float32),
        "ew": ew.astype(np.float32), "jw": jw.astype(np.float32),
    }

def reference(tab_words, tab_scales, offs, pos1, pos2, w1, w4_words, w4_scales, gain, prof, ew, jw):
    v = unpack_weight(tab_words, tab_scales, "e4m3")[:, unstriped(offs)]
    w4 = unpack_weight(w4_words, w4_scales, "e2m1")
    h = np.tanh(mxq(f64(w1), 0, "e4m3").T @ v) * f64(gain)[:, None]
    x1 = h[:, unstriped(pos1)] - f64(prof)[:, None]
    x2 = np.abs(h[:, unstriped(pos2)] - f64(prof)[:, None]) * f64(ew)[:, None]
    q1 = mxq(x1, 0, "e4m3")
    q2 = mxq(x2, 0, "e4m3")
    e = q1.T @ q2 + q1.T @ w4
    return e * f64(jw)[None, :]

@@ -1,0 +1,253 @@
+from contextlib import ExitStack
+
+import concourse.mybir as mybir
+
+K, H, T, S, NP = 1536, 1024, 2048, 1024, 512
+FLOPS = 2 * K * H * S + 4 * H * NP * NP
+
+F32 = mybir.dt.float32
+BF16 = mybir.dt.bfloat16
+I32 = mybir.dt.int32
+U32 = mybir.dt.uint32
+U16 = mybir.dt.uint16
+U8 = mybir.dt.uint8
+FP8X4 = mybir.dt.float8_e4m3fn_x4
+FP4X4 = mybir.dt.float4_e2m1fn_x4
+ACT = mybir.ActivationFunctionType
+ALU = mybir.AluOpType
+
+P = 128
+PACK = 4
+KP = P * PACK
+KA = K // KP
+RB = H // KP
+BANK = 512
+
+
+def tile_list_tablet_join_scores_kernel(
+    tc, tab_words, tab_scales, offs, pos1, pos2, w1, w4_words, w4_scales, gain, prof, ew, jw, out
+):
+    nc = tc.nc
+    with ExitStack() as ctx:
+        keep = ctx.enter_context(tc.tile_pool(name="keep", bufs=1))
+        ring = ctx.enter_context(tc.tile_pool(name="ring", bufs=1))
+        psum = ctx.enter_context(tc.psum_pool(name="psum", bufs=1))
+
+        offs_sb = keep.tile([P, S // 16], U16, name="offs_sb")
+        pos1_sb = keep.tile([P, NP // 16], U16, name="pos1_sb")
+        pos2_sb = keep.tile([P, NP // 16], U16, name="pos2_sb")
+        nc.sync.dma_start(offs_sb[:], offs)
+
+        tscale = keep.tile([P, T], U8, name="tscale", align_bytes=64)
+        nc.vector.memset(tscale[:].bitcast(I32), 0)
+        for q in range(4):
+            nc.scalar.dma_start(
+                tscale[32 * q : 32 * q + 4 * KA, :].bitcast(I32),
+                tab_scales[:, 4 * q : 4 * q + 4, :].bitcast(I32),
+            )
+
+        gain_sb = keep.tile([P, RB, PACK], F32, name="gain_sb")
+        prof_sb = keep.tile([P, RB, PACK], F32, name="prof_sb")
+        ew_sb = keep.tile([P, RB, PACK], F32, name="ew_sb")
+        nprof = keep.tile([P, RB, PACK], F32, name="nprof")
+
+        twords = []
+        raws = {}
+
+        def load_table(a):
+            tw = keep.tile([P, T], I32, name=f"twords{a}", align_bytes=64)
+            nc.sync.dma_start(tw[:], tab_words[a].rearrange("p t i -> p (t i)").bitcast(I32))
+            twords.append(tw)
+
+        def load_w1(a, b, c0, c1, tag, bufs):
+            raw = ring.tile([P, PACK, c1 - c0], F32, name=f"raw{a}{b}{c0}", tag=tag, bufs=bufs)
+            rows = w1[KP * a : KP * (a + 1), KP * b + c0 : KP * b + c1]
+            nc.sync.dma_start(raw[:], rows.rearrange("(p j) c -> p j c", j=PACK))
+            raws[a, b, c0] = raw
+
+        for a in range(KA):
+            load_table(a)
+            if a < KA - 1:
+                load_w1(a, 0, 0, KP, "raw", 4)
+        load_w1(KA - 1, 0, 0, KP // 2, "rawh", 2)
+        load_w1(KA - 1, 0, KP // 2, KP, "rawh", 2)
+        for dst, src in ((prof_sb, prof), (gain_sb, gain)):
+            nc.sync.dma_start(dst[:], src.rearrange("(b p t) -> p b t", p=P, t=PACK))
+        nc.sync.dma_start(pos2_sb[:], pos2)
+        nc.sync.dma_start(pos1_sb[:], pos1)
+        for a in range(KA):
+            load_w1(a, 1, 0, KP, "raw", 4)
+
+        nc.sync.dma_start(ew_sb[:], ew.rearrange("(b p t) -> p b t", p=P, t=PACK))
+        w4w = keep.tile([P, RB, 2 * NP], U8, name="w4w", align_bytes=64)
+        nc.sync.dma_start(w4w[:].bitcast(I32), w4_words.rearrange("a p c -> p a c").bitcast(I32))
+        w4s = keep.tile([P, RB, NP], U8, name="w4s", align_bytes=64)
+        nc.gpsimd.memset(w4s[:].bitcast(I32), 0)
+        for q in range(4):
+            nc.sync.dma_start(
+                w4s[32 * q : 32 * q + 4, :, :].bitcast(I32),
+                w4_scales[:, 4 * q : 4 * q + 4, :].rearrange("a r c -> r a c").bitcast(I32),
+            )
+        jw_sb = keep.tile([P, NP], F32, name="jw_sb")
+        nc.sync.dma_start(jw_sb[:], jw.partition_broadcast(P))
+
+        nc.gpsimd.tensor_scalar(nprof[:], prof_sb[:], -1.0, 0.0, ALU.mult, ALU.add)
+
+        vscale = keep.tile([P, S], U8, name="vscale", align_bytes=64)
+        nc.vector.tensor_copy(vscale[:], tscale[:].indirect(offs_sb[:]))
+        vwords = []
+
+        def gather_table(a):
+            vw = keep.tile([P, S], U32, name=f"vwords{a}", align_bytes=64)
+            nc.vector.tensor_copy(vw[:], twords[a][:].bitcast(U32).indirect(offs_sb[:]))
+            vwords.append(vw)
+
+        def cast_w1(copy, grouped, raw, c0, lo, hi):
+            m0, m1 = (c0 + lo) // PACK, (c0 + hi) // PACK
+            dst = grouped[:].rearrange("p (t m j) -> p m j t", t=PACK, j=PACK)[:, m0:m1]
+            copy(dst, raw[:, :, lo:hi].rearrange("p j (m t) -> p m j t", t=PACK))
+
+        wq = {}
+
+        def quantise(name, grouped, cuts):
+            width = grouped.shape[1] // PACK
+            codes = keep.tile([P, width], U32, name=f"{name}_codes", align_bytes=64)
+            scales = keep.tile([P, width], U8, name=f"{name}_scales", align_bytes=64)
+            for c0, c1 in zip(cuts, cuts[1:]):
+                nc.vector.quantize_mx(
+                    out=codes[:, c0:c1].bitcast(FP8X4), scales=scales[:, c0:c1], in_=grouped[:, PACK * c0 : PACK * c1]
+                )
+            return codes, scales
+
+        def new_grouped(a, b):
+            return ring.tile([P, PACK * KP], BF16, name=f"grouped{a}{b}", tag="grouped", bufs=3, align_bytes=64)
+
+        banks = {}
+
+        def stage1_pass(a, b, t):
+            codes, scales = wq[a, b]
+            for half in range(2):
+                if a == 0:
+                    banks[b, t, half] = psum.tile([P, BANK], F32, name=f"acc{b}{t}{half}", tag=f"bank{2 * t + half}")
+                cols = slice(BANK * half, BANK * (half + 1))
+                nc.tensor.matmul_mx(
+                    out=banks[b, t, half][:],
+                    lhsT=codes[:, P * t : P * (t + 1)].bitcast(FP8X4),
+                    lhsT_scale=scales[:, P * t : P * (t + 1)],
+                    rhs=vwords[a][:, cols].bitcast(FP8X4),
+                    rhs_scale=vscale[4 * a :, cols],
+                    start=(a == 0),
+                    stop=(a == KA - 1),
+                )
+
+        hs = {}
+
+        def tanh_slice(b, t):
+            h = keep.tile([P, S], F32, name=f"h{b}{t}")
+            for half in range(2):
+                nc.scalar.activation(h[:, BANK * half : BANK * (half + 1)], banks[b, t, half][:], ACT.Tanh)
+            hs[b, t] = h
+
+        def pick(dst, b, t, pos_sb, c0, c1, func):
+            nc.vector.tensor_copy(dst[:, t, c0:c1], hs[b, t][:].indirect(pos_sb[:, c0 // 16 : c1 // 16]))
+            nc.scalar.activation(
+                dst[:, t, c0:c1], dst[:, t, c0:c1], func, bias=nprof[:, b, t : t + 1], scale=gain_sb[:, b, t : t + 1]
+            )
+
+        def woven(grouped, c0, c1):
+            return grouped[:, PACK * c0 : PACK * c1].rearrange("p (c i t) -> p c t i", i=4, t=PACK)
+
+        def planes(x, c0, c1):
+            return x[:, :, c0:c1].rearrange("p t (c i) -> p c t i", i=4)
+
+        for a in range(KA):
+            gather_table(a)
+            grouped = new_grouped(a, 0)
+            if a < KA - 1:
+                cast_w1(nc.scalar.copy, grouped, raws[a, 0, 0], 0, 0, KP)
+                wq[a, 0] = quantise(f"w{a}0", grouped, [0, KP])
+            else:
+                cast_w1(nc.scalar.copy, grouped, raws[a, 0, 0], 0, 0, KP // 2)
+                cast_w1(nc.vector.tensor_copy, grouped, raws[a, 0, KP // 2], KP // 2, 0, KP // 2)
+                wq[a, 0] = quantise(f"w{a}0", grouped, [0, P, KP])
+            for t in range(PACK):
+                stage1_pass(a, 0, t)
+
+        x1 = [keep.tile([P, PACK, NP], F32, name=f"x1_{b}") for b in range(RB)]
+        x2 = [keep.tile([P, PACK, NP], F32, name=f"x2_{b}") for b in range(RB)]
+        x1g = [keep.tile([P, PACK * NP], BF16, name=f"x1g{b}", align_bytes=64) for b in range(RB)]
+        x2g = [keep.tile([P, PACK * NP], BF16, name=f"x2g{b}", align_bytes=64) for b in range(RB)]
+
+        def weigh_x2(b):
+            ew_b = ew_sb[:, b, :].unsqueeze(1).unsqueeze(3).to_broadcast([P, NP // 4, PACK, 4])
+            nc.vector.tensor_tensor(woven(x2g[b], 0, NP), planes(x2[b], 0, NP), ew_b, ALU.mult)
+
+        for t in range(PACK):
+            tanh_slice(0, t)
+            pick(x2[0], 0, t, pos2_sb, 0, NP, ACT.Abs)
+            pick(x1[0], 0, t, pos1_sb, 0, NP, ACT.Identity)
+            if t > 0:
+                a = t - 1
+                grouped = new_grouped(a, 1)
+                cast_w1(nc.scalar.copy, grouped, raws[a, 1, 0], 0, 0, KP)
+                wq[a, 1] = quantise(f"w{a}1", grouped, [0, KP])
+                for u in range(PACK):
+                    stage1_pass(a, 1, u)
+
+        q1, q2 = {}, {}
+        for t in range(PACK):
+            tanh_slice(1, t)
+        weigh_x2(0)
+        nc.scalar.copy(woven(x1g[0], 0, NP), planes(x1[0], 0, NP))
+        q2[0] = quantise("q20", x2g[0], [0, NP])
+        for t in range(PACK):
+            pick(x2[1], 1, t, pos2_sb, 0, NP, ACT.Abs)
+        q1[0] = quantise("q10", x1g[0], [0, NP])
+
+        scores = [psum.tile([P, NP], F32, name=f"score{i}", tag=f"bank{i}") for i in range(NP // P)]
+
+        def stage2_passes(b, i):
+            codes, scales = q1[b]
+            rows = slice(P * i, P * (i + 1))
+            nc.tensor.matmul_mx(
+                out=scores[i][:],
+                lhsT=codes[:, rows].bitcast(FP8X4),
+                lhsT_scale=scales[:, rows],
+                rhs=w4w[:, b, :].bitcast(FP4X4),
+                rhs_scale=w4s[:, b, :],
+                start=(b == 0),
+                stop=False,
+            )
+            nc.tensor.matmul_mx(
+                out=scores[i][:],
+                lhsT=codes[:, rows].bitcast(FP8X4),
+                lhsT_scale=scales[:, rows],
+                rhs=q2[b][0][:].bitcast(FP8X4),
+                rhs_scale=q2[b][1][:],
+                start=False,
+                stop=(b == RB - 1),
+            )
+
+        for i in range(NP // P):
+            stage2_passes(0, i)
+
+        codes1 = keep.tile([P, NP], U32, name="q11_codes", align_bytes=64)
+        scales1 = keep.tile([P, NP], U8, name="q11_scales", align_bytes=64)
+        q1[1] = (codes1, scales1)
+        cuts = [0, 256, 384, 512]
+        for n, (c0, c1) in enumerate(zip(cuts, cuts[1:])):
+            for t in range(PACK):
+                pick(x1[1], 1, t, pos1_sb, c0, c1, ACT.Identity)
+            if n == 0:
+                weigh_x2(1)
+                q2[1] = quantise("q21", x2g[1], [0, NP])
+            nc.scalar.copy(woven(x1g[1], c0, c1), planes(x1[1], c0, c1))
+        for c0, c1 in zip(cuts, cuts[1:]):
+            nc.vector.quantize_mx(
+                out=codes1[:, c0:c1].bitcast(FP8X4), scales=scales1[:, c0:c1], in_=x1g[1][:, PACK * c0 : PACK * c1]
+            )
+            for i in range(c0 // P, c1 // P):
+                stage2_passes(1, i)
+                res = keep.tile([P, NP], F32, name=f"res{i}")
+                nc.vector.tensor_tensor(res[:], scores[i][:], jw_sb[:], ALU.mult)
+                nc.sync.dma_start(out[P * i : P * (i + 1), :], res[:])

@@ -18,10 +18,16 @@ ALU = mybir.AluOpType
 
 P = 128
 PACK = 4
-KP = P * PACK
-KA = K // KP
-RB = H // KP
+PASS = P * PACK
+K_PASSES = K // PASS
+R_PASSES = H // PASS
 BANK = 512
+QUADRANT = 32
+PER_COLUMN = 16
+LAST = PACK - 1
+HALVES = ((0, NP // 2), (NP // 2, NP))
+
+SCALAR_COLUMNS = {(0, 0): PASS, (1, 0): 192, (2, 0): 160, (0, 1): 0, (1, 1): PASS, (2, 1): PASS}
 
 
 def tile_list_tablet_join_scores_kernel(
@@ -30,224 +36,230 @@ def tile_list_tablet_join_scores_kernel(
     nc = tc.nc
     with ExitStack() as ctx:
         keep = ctx.enter_context(tc.tile_pool(name="keep", bufs=1))
-        ring = ctx.enter_context(tc.tile_pool(name="ring", bufs=1))
+        ring = ctx.enter_context(tc.tile_pool(name="ring", bufs=3))
         psum = ctx.enter_context(tc.psum_pool(name="psum", bufs=1))
 
-        offs_sb = keep.tile([P, S // 16], U16, name="offs_sb")
-        pos1_sb = keep.tile([P, NP // 16], U16, name="pos1_sb")
-        pos2_sb = keep.tile([P, NP // 16], U16, name="pos2_sb")
+        offs_sb = keep.tile([P, S // PER_COLUMN], U16, name="offs_sb")
+        pos1_sb = keep.tile([P, NP // PER_COLUMN], U16, name="pos1_sb")
+        pos2_sb = keep.tile([P, NP // PER_COLUMN], U16, name="pos2_sb")
         nc.sync.dma_start(offs_sb[:], offs)
 
-        tscale = keep.tile([P, T], U8, name="tscale", align_bytes=64)
-        nc.vector.memset(tscale[:].bitcast(I32), 0)
-        for q in range(4):
-            nc.scalar.dma_start(
-                tscale[32 * q : 32 * q + 4 * KA, :].bitcast(I32),
-                tab_scales[:, 4 * q : 4 * q + 4, :].bitcast(I32),
-            )
+        tab_scale_sb = keep.tile([P, T], U8, name="tab_scale_sb", align_bytes=64)
+        w4_scale_sb = keep.tile([P, R_PASSES, NP], U8, name="w4_scale_sb", align_bytes=64)
+        nc.gpsimd.memset(tab_scale_sb[:].bitcast(I32), 0)
+        nc.gpsimd.memset(w4_scale_sb[:].bitcast(I32), 0)
 
-        gain_sb = keep.tile([P, RB, PACK], F32, name="gain_sb")
-        prof_sb = keep.tile([P, RB, PACK], F32, name="prof_sb")
-        ew_sb = keep.tile([P, RB, PACK], F32, name="ew_sb")
-        nprof = keep.tile([P, RB, PACK], F32, name="nprof")
-
-        twords = []
-        raws = {}
-
-        def load_table(a):
-            tw = keep.tile([P, T], I32, name=f"twords{a}", align_bytes=64)
-            nc.sync.dma_start(tw[:], tab_words[a].rearrange("p t i -> p (t i)").bitcast(I32))
-            twords.append(tw)
-
-        def load_w1(a, b, c0, c1, tag, bufs):
-            raw = ring.tile([P, PACK, c1 - c0], F32, name=f"raw{a}{b}{c0}", tag=tag, bufs=bufs)
-            rows = w1[KP * a : KP * (a + 1), KP * b + c0 : KP * b + c1]
-            nc.sync.dma_start(raw[:], rows.rearrange("(p j) c -> p j c", j=PACK))
-            raws[a, b, c0] = raw
-
-        for a in range(KA):
-            load_table(a)
-            if a < KA - 1:
-                load_w1(a, 0, 0, KP, "raw", 4)
-        load_w1(KA - 1, 0, 0, KP // 2, "rawh", 2)
-        load_w1(KA - 1, 0, KP // 2, KP, "rawh", 2)
-        for dst, src in ((prof_sb, prof), (gain_sb, gain)):
-            nc.sync.dma_start(dst[:], src.rearrange("(b p t) -> p b t", p=P, t=PACK))
+        tab_word_sb = []
+        for a in range(K_PASSES):
+            words = keep.tile([P, T], I32, name=f"tab_word_sb{a}", align_bytes=64)
+            nc.sync.dma_start(words[:], tab_words[a].rearrange("p t i -> p (t i)").bitcast(I32))
+            tab_word_sb.append(words)
         nc.sync.dma_start(pos2_sb[:], pos2)
-        nc.sync.dma_start(pos1_sb[:], pos1)
-        for a in range(KA):
-            load_w1(a, 1, 0, KP, "raw", 4)
+        for q in range(P // QUADRANT):
+            rows = slice(QUADRANT * q, QUADRANT * q + 4 * K_PASSES)
+            nc.sync.dma_start(tab_scale_sb[rows, :].bitcast(I32), tab_scales[:, 4 * q : 4 * q + 4, :].bitcast(I32))
 
-        nc.sync.dma_start(ew_sb[:], ew.rearrange("(b p t) -> p b t", p=P, t=PACK))
-        w4w = keep.tile([P, RB, 2 * NP], U8, name="w4w", align_bytes=64)
-        nc.sync.dma_start(w4w[:].bitcast(I32), w4_words.rearrange("a p c -> p a c").bitcast(I32))
-        w4s = keep.tile([P, RB, NP], U8, name="w4s", align_bytes=64)
-        nc.gpsimd.memset(w4s[:].bitcast(I32), 0)
-        for q in range(4):
+        w1_sb = {}
+        for b in range(R_PASSES):
+            for a in range(K_PASSES):
+                w1_sb[a, b] = keep.tile([P, PACK, PASS], F32, name=f"w1_sb{a}{b}")
+                piece = w1[PASS * a : PASS * (a + 1), PASS * b : PASS * (b + 1)]
+                nc.sync.dma_start(w1_sb[a, b][:], piece.rearrange("(p j) c -> p j c", j=PACK))
+            if b == 0:
+                nc.sync.dma_start(pos1_sb[:], pos1)
+
+        gain_sb = keep.tile([P, R_PASSES, PACK], F32, name="gain_sb")
+        prof_sb = keep.tile([P, R_PASSES, PACK], F32, name="prof_sb")
+        ew_sb = keep.tile([P, R_PASSES, PACK], F32, name="ew_sb")
+        for dst, src in ((prof_sb, prof), (gain_sb, gain), (ew_sb, ew)):
+            nc.sync.dma_start(dst[:], src.rearrange("(b p t) -> p b t", p=P, t=PACK))
+        for q in range(P // QUADRANT):
             nc.sync.dma_start(
-                w4s[32 * q : 32 * q + 4, :, :].bitcast(I32),
-                w4_scales[:, 4 * q : 4 * q + 4, :].rearrange("a r c -> r a c").bitcast(I32),
+                w4_scale_sb[QUADRANT * q : QUADRANT * q + 4, :, :].bitcast(I32),
+                w4_scales[:, 4 * q : 4 * q + 4, :].rearrange("b r c -> r b c").bitcast(I32),
             )
+        w4_word_sb = keep.tile([P, R_PASSES, 2 * NP], U8, name="w4_word_sb", align_bytes=64)
+        nc.sync.dma_start(w4_word_sb[:].bitcast(I32), w4_words.rearrange("b p c -> p b c").bitcast(I32))
         jw_sb = keep.tile([P, NP], F32, name="jw_sb")
         nc.sync.dma_start(jw_sb[:], jw.partition_broadcast(P))
 
-        nc.gpsimd.tensor_scalar(nprof[:], prof_sb[:], -1.0, 0.0, ALU.mult, ALU.add)
+        minus_prof = keep.tile([P, R_PASSES, PACK], F32, name="minus_prof")
+        ew_gain = keep.tile([P, R_PASSES, PACK], F32, name="ew_gain")
+        minus_ew_prof = keep.tile([P, R_PASSES, PACK], F32, name="minus_ew_prof")
+        ew_sign = keep.tile([P, R_PASSES, PACK], F32, name="ew_sign")
+        nc.gpsimd.tensor_scalar(minus_prof[:], prof_sb[:], -1.0, 0.0, ALU.mult, ALU.add)
+        nc.gpsimd.tensor_tensor(ew_gain[:], ew_sb[:], gain_sb[:], ALU.mult)
+        nc.gpsimd.tensor_tensor(minus_ew_prof[:], ew_sb[:], minus_prof[:], ALU.mult)
+        nc.gpsimd.tensor_scalar(ew_sign[:], ew_sb[:], 0.0, 2.0, ALU.is_ge, ALU.mult)
+        nc.gpsimd.tensor_scalar(ew_sign[:], ew_sign[:], 1.0, -1.0, ALU.mult, ALU.add)
 
-        vscale = keep.tile([P, S], U8, name="vscale", align_bytes=64)
-        nc.vector.tensor_copy(vscale[:], tscale[:].indirect(offs_sb[:]))
-        vwords = []
-
-        def gather_table(a):
-            vw = keep.tile([P, S], U32, name=f"vwords{a}", align_bytes=64)
-            nc.vector.tensor_copy(vw[:], twords[a][:].bitcast(U32).indirect(offs_sb[:]))
-            vwords.append(vw)
-
-        def cast_w1(copy, grouped, raw, c0, lo, hi):
-            m0, m1 = (c0 + lo) // PACK, (c0 + hi) // PACK
-            dst = grouped[:].rearrange("p (t m j) -> p m j t", t=PACK, j=PACK)[:, m0:m1]
-            copy(dst, raw[:, :, lo:hi].rearrange("p j (m t) -> p m j t", t=PACK))
-
-        wq = {}
-
-        def quantise(name, grouped, cuts):
-            width = grouped.shape[1] // PACK
-            codes = keep.tile([P, width], U32, name=f"{name}_codes", align_bytes=64)
-            scales = keep.tile([P, width], U8, name=f"{name}_scales", align_bytes=64)
-            for c0, c1 in zip(cuts, cuts[1:]):
-                nc.vector.quantize_mx(
-                    out=codes[:, c0:c1].bitcast(FP8X4), scales=scales[:, c0:c1], in_=grouped[:, PACK * c0 : PACK * c1]
-                )
+        def mx_tiles(name):
+            codes = keep.tile([P, PASS], U32, name=f"{name}_codes", align_bytes=64)
+            scales = keep.tile([P, PASS], U8, name=f"{name}_scales", align_bytes=64)
             return codes, scales
 
-        def new_grouped(a, b):
-            return ring.tile([P, PACK * KP], BF16, name=f"grouped{a}{b}", tag="grouped", bufs=3, align_bytes=64)
+        def quantise(mx, rounded, c0=0, c1=PASS):
+            codes, scales = mx
+            nc.vector.quantize_mx(
+                out=codes[:, c0:c1].bitcast(FP8X4), scales=scales[:, c0:c1], in_=rounded[:, PACK * c0 : PACK * c1]
+            )
 
-        banks = {}
+        v_words = []
+        for a in range(K_PASSES):
+            picked_words = keep.tile([P, S], U32, name=f"v_words{a}", align_bytes=64)
+            nc.vector.tensor_copy(picked_words[:], tab_word_sb[a][:].bitcast(U32).indirect(offs_sb[:]))
+            v_words.append(picked_words)
+        v_scales = keep.tile([P, S], U8, name="v_scales", align_bytes=64)
+        nc.vector.tensor_copy(v_scales[:], tab_scale_sb[:].indirect(offs_sb[:]))
 
-        def stage1_pass(a, b, t):
-            codes, scales = wq[a, b]
-            for half in range(2):
-                if a == 0:
-                    banks[b, t, half] = psum.tile([P, BANK], F32, name=f"acc{b}{t}{half}", tag=f"bank{2 * t + half}")
-                cols = slice(BANK * half, BANK * (half + 1))
-                nc.tensor.matmul_mx(
-                    out=banks[b, t, half][:],
-                    lhsT=codes[:, P * t : P * (t + 1)].bitcast(FP8X4),
-                    lhsT_scale=scales[:, P * t : P * (t + 1)],
-                    rhs=vwords[a][:, cols].bitcast(FP8X4),
-                    rhs_scale=vscale[4 * a :, cols],
-                    start=(a == 0),
-                    stop=(a == KA - 1),
-                )
+        w1_mx = {}
 
-        hs = {}
+        def prepare_w1(a, b):
+            rounded = ring.tile([P, PACK * PASS], BF16, name=f"w1_rounded{a}{b}", tag="w1_rounded", align_bytes=64)
+            dst = rounded[:].rearrange("p (t m u e) -> p m u t e", t=PACK, u=2, e=2)
+            src = w1_sb[a, b][:].rearrange("p (u e) (m t) -> p m u t e", e=2, t=PACK)
+            split = SCALAR_COLUMNS[a, b] // PACK
+            if split > 0:
+                nc.scalar.copy(dst[:, :split], src[:, :split])
+            if split < P:
+                nc.vector.tensor_copy(dst[:, split:], src[:, split:])
+            w1_mx[a, b] = mx_tiles(f"w1_{a}{b}")
+            if (a, b) == (K_PASSES - 1, 0):
+                quantise(w1_mx[a, b], rounded, 0, P)
+                quantise(w1_mx[a, b], rounded, P, PASS)
+            else:
+                quantise(w1_mx[a, b], rounded)
+
+        sums = {}
+
+        def first_stage(b):
+            for t in range(PACK):
+                for half in range(S // BANK):
+                    sums[b, t, half] = psum.tile([P, BANK], F32, name=f"sums{b}{t}{half}", tag=f"bank{2 * t + half}")
+                for a in range(K_PASSES):
+                    codes, scales = w1_mx[a, b]
+                    for half in range(S // BANK):
+                        cols = slice(BANK * half, BANK * (half + 1))
+                        nc.tensor.matmul_mx(
+                            out=sums[b, t, half][:],
+                            lhsT=codes[:, P * t : P * (t + 1)].bitcast(FP8X4),
+                            lhsT_scale=scales[:, P * t : P * (t + 1)],
+                            rhs=v_words[a][:, cols].bitcast(FP8X4),
+                            rhs_scale=v_scales[4 * a :, cols],
+                            start=(a == 0),
+                            stop=(a == K_PASSES - 1),
+                        )
+
+        upper = [keep.tile([P, PACK, NP], F32, name=f"upper{b}") for b in range(R_PASSES)]
+        lower = [keep.tile([P, PACK, NP], F32, name=f"lower{b}") for b in range(R_PASSES)]
+        x1_rows = [keep.tile([P, PACK, NP], BF16, name=f"x1_rows{b}") for b in range(R_PASSES)]
+        x2_rows = [keep.tile([P, PACK, NP], BF16, name=f"x2_rows{b}") for b in range(R_PASSES)]
+        x1_woven = [keep.tile([P, PACK * NP], BF16, name=f"x1_woven{b}", align_bytes=64) for b in range(R_PASSES)]
+        x2_woven = [keep.tile([P, PACK * NP], BF16, name=f"x2_woven{b}", align_bytes=64) for b in range(R_PASSES)]
+        x1_mx = [mx_tiles(f"x1_{b}") for b in range(R_PASSES)]
+        x2_mx = [mx_tiles(f"x2_{b}") for b in range(R_PASSES)]
+        tanh_sb = {}
 
         def tanh_slice(b, t):
-            h = keep.tile([P, S], F32, name=f"h{b}{t}")
-            for half in range(2):
-                nc.scalar.activation(h[:, BANK * half : BANK * (half + 1)], banks[b, t, half][:], ACT.Tanh)
-            hs[b, t] = h
+            tanh_sb[b, t] = keep.tile([P, S], F32, name=f"tanh_sb{b}{t}")
+            for half in range(S // BANK):
+                nc.scalar.activation(tanh_sb[b, t][:, BANK * half : BANK * (half + 1)], sums[b, t, half][:], ACT.Tanh)
 
-        def pick(dst, b, t, pos_sb, c0, c1, func):
-            nc.vector.tensor_copy(dst[:, t, c0:c1], hs[b, t][:].indirect(pos_sb[:, c0 // 16 : c1 // 16]))
+        def pick(dst, pos_sb, b, t, c0=0, c1=NP):
+            offsets = pos_sb[:, c0 // PER_COLUMN : c1 // PER_COLUMN]
+            nc.vector.tensor_copy(dst[b][:, t, c0:c1], tanh_sb[b, t][:].indirect(offsets))
+
+        def tanh_and_pick(b, t):
+            tanh_slice(b, t)
+            pick(lower, pos2_sb, b, t)
+            pick(upper, pos1_sb, b, t)
+
+        def make_x1(b, t):
             nc.scalar.activation(
-                dst[:, t, c0:c1], dst[:, t, c0:c1], func, bias=nprof[:, b, t : t + 1], scale=gain_sb[:, b, t : t + 1]
+                x1_rows[b][:, t, :],
+                upper[b][:, t, :],
+                ACT.Identity,
+                bias=minus_prof[:, b, t : t + 1],
+                scale=gain_sb[:, b, t : t + 1],
             )
 
-        def woven(grouped, c0, c1):
-            return grouped[:, PACK * c0 : PACK * c1].rearrange("p (c i t) -> p c t i", i=4, t=PACK)
-
-        def planes(x, c0, c1):
-            return x[:, :, c0:c1].rearrange("p t (c i) -> p c t i", i=4)
-
-        for a in range(KA):
-            gather_table(a)
-            grouped = new_grouped(a, 0)
-            if a < KA - 1:
-                cast_w1(nc.scalar.copy, grouped, raws[a, 0, 0], 0, 0, KP)
-                wq[a, 0] = quantise(f"w{a}0", grouped, [0, KP])
-            else:
-                cast_w1(nc.scalar.copy, grouped, raws[a, 0, 0], 0, 0, KP // 2)
-                cast_w1(nc.vector.tensor_copy, grouped, raws[a, 0, KP // 2], KP // 2, 0, KP // 2)
-                wq[a, 0] = quantise(f"w{a}0", grouped, [0, P, KP])
-            for t in range(PACK):
-                stage1_pass(a, 0, t)
-
-        x1 = [keep.tile([P, PACK, NP], F32, name=f"x1_{b}") for b in range(RB)]
-        x2 = [keep.tile([P, PACK, NP], F32, name=f"x2_{b}") for b in range(RB)]
-        x1g = [keep.tile([P, PACK * NP], BF16, name=f"x1g{b}", align_bytes=64) for b in range(RB)]
-        x2g = [keep.tile([P, PACK * NP], BF16, name=f"x2g{b}", align_bytes=64) for b in range(RB)]
-
-        def weigh_x2(b):
-            ew_b = ew_sb[:, b, :].unsqueeze(1).unsqueeze(3).to_broadcast([P, NP // 4, PACK, 4])
-            nc.vector.tensor_tensor(woven(x2g[b], 0, NP), planes(x2[b], 0, NP), ew_b, ALU.mult)
-
-        for t in range(PACK):
-            tanh_slice(0, t)
-            pick(x2[0], 0, t, pos2_sb, 0, NP, ACT.Abs)
-            pick(x1[0], 0, t, pos1_sb, 0, NP, ACT.Identity)
-            if t > 0:
-                a = t - 1
-                grouped = new_grouped(a, 1)
-                cast_w1(nc.scalar.copy, grouped, raws[a, 1, 0], 0, 0, KP)
-                wq[a, 1] = quantise(f"w{a}1", grouped, [0, KP])
-                for u in range(PACK):
-                    stage1_pass(a, 1, u)
-
-        q1, q2 = {}, {}
-        for t in range(PACK):
-            tanh_slice(1, t)
-        weigh_x2(0)
-        nc.scalar.copy(woven(x1g[0], 0, NP), planes(x1[0], 0, NP))
-        q2[0] = quantise("q20", x2g[0], [0, NP])
-        for t in range(PACK):
-            pick(x2[1], 1, t, pos2_sb, 0, NP, ACT.Abs)
-        q1[0] = quantise("q10", x1g[0], [0, NP])
-
-        scores = [psum.tile([P, NP], F32, name=f"score{i}", tag=f"bank{i}") for i in range(NP // P)]
-
-        def stage2_passes(b, i):
-            codes, scales = q1[b]
-            rows = slice(P * i, P * (i + 1))
-            nc.tensor.matmul_mx(
-                out=scores[i][:],
-                lhsT=codes[:, rows].bitcast(FP8X4),
-                lhsT_scale=scales[:, rows],
-                rhs=w4w[:, b, :].bitcast(FP4X4),
-                rhs_scale=w4s[:, b, :],
-                start=(b == 0),
-                stop=False,
+        def make_x2(b, t, c0=0, c1=NP):
+            x2 = x2_rows[b][:, t, c0:c1]
+            nc.scalar.activation(
+                x2, lower[b][:, t, c0:c1], ACT.Abs, bias=minus_ew_prof[:, b, t : t + 1], scale=ew_gain[:, b, t : t + 1]
             )
-            nc.tensor.matmul_mx(
-                out=scores[i][:],
-                lhsT=codes[:, rows].bitcast(FP8X4),
-                lhsT_scale=scales[:, rows],
-                rhs=q2[b][0][:].bitcast(FP8X4),
-                rhs_scale=q2[b][1][:],
-                start=False,
-                stop=(b == RB - 1),
+            nc.vector.tensor_scalar(x2, x2, ew_sign[:, b, t : t + 1], None, ALU.mult)
+
+        def weave(copy, woven, rows, c0=0, c1=NP):
+            copy(
+                woven[:, PACK * c0 : PACK * c1].rearrange("p (c t) -> p c t", t=PACK),
+                rows[:, :, c0:c1].rearrange("p t c -> p c t"),
             )
+
+        for a in range(K_PASSES):
+            prepare_w1(a, 0)
+        first_stage(0)
+        prepare_w1(0, 1)
+        tanh_and_pick(0, 0)
+        for t in range(1, LAST):
+            tanh_and_pick(0, t)
+            prepare_w1(t, 1)
+        tanh_and_pick(0, LAST)
+
+        first_stage(1)
+        for t in range(LAST):
+            make_x2(0, t)
+        tanh_and_pick(1, 0)
+        make_x2(0, LAST)
+        make_x1(0, 0)
+        weave(nc.vector.tensor_copy, x2_woven[0], x2_rows[0])
+        quantise(x2_mx[0], x2_woven[0])
+        tanh_and_pick(1, 1)
+        for t in range(1, PACK):
+            make_x1(0, t)
+        tanh_and_pick(1, 2)
+        tanh_slice(1, LAST)
+        pick(upper, pos1_sb, 1, LAST)
+        for c0, c1 in HALVES:
+            pick(lower, pos2_sb, 1, LAST, c0, c1)
+        weave(nc.scalar.copy, x1_woven[0], x1_rows[0])
+        quantise(x1_mx[0], x1_woven[0])
+
+        scores = [psum.tile([P, NP], F32, name=f"scores{i}", tag=f"bank{i}") for i in range(NP // P)]
+
+        def second_stage(b):
+            codes, scales = x1_mx[b]
+            w4_operand = (w4_word_sb[:, b, :].bitcast(FP4X4), w4_scale_sb[:, b, :])
+            x2_operand = (x2_mx[b][0][:].bitcast(FP8X4), x2_mx[b][1][:])
+            for i in range(NP // P):
+                rows = slice(P * i, P * (i + 1))
+                for n, (rhs, rhs_scale) in enumerate((w4_operand, x2_operand)):
+                    nc.tensor.matmul_mx(
+                        out=scores[i][:],
+                        lhsT=codes[:, rows].bitcast(FP8X4),
+                        lhsT_scale=scales[:, rows],
+                        rhs=rhs,
+                        rhs_scale=rhs_scale,
+                        start=(b == 0 and n == 0),
+                        stop=(b == R_PASSES - 1 and n == 1),
+                    )
+
+        second_stage(0)
+        for t in range(LAST):
+            make_x2(1, t)
+        for t in range(LAST):
+            make_x1(1, t)
+        for c0, c1 in HALVES:
+            make_x2(1, LAST, c0, c1)
+            weave(nc.vector.tensor_copy, x2_woven[1], x2_rows[1], c0, c1)
+        quantise(x2_mx[1], x2_woven[1])
+        make_x1(1, LAST)
+        for c0, c1 in HALVES:
+            weave(nc.scalar.copy, x1_woven[1], x1_rows[1], c0, c1)
+            quantise(x1_mx[1], x1_woven[1], c0, c1)
+        second_stage(1)
 
         for i in range(NP // P):
-            stage2_passes(0, i)
-
-        codes1 = keep.tile([P, NP], U32, name="q11_codes", align_bytes=64)
-        scales1 = keep.tile([P, NP], U8, name="q11_scales", align_bytes=64)
-        q1[1] = (codes1, scales1)
-        cuts = [0, 256, 384, 512]
-        for n, (c0, c1) in enumerate(zip(cuts, cuts[1:])):
-            for t in range(PACK):
-                pick(x1[1], 1, t, pos1_sb, c0, c1, ACT.Identity)
-            if n == 0:
-                weigh_x2(1)
-                q2[1] = quantise("q21", x2g[1], [0, NP])
-            nc.scalar.copy(woven(x1g[1], c0, c1), planes(x1[1], c0, c1))
-        for c0, c1 in zip(cuts, cuts[1:]):
-            nc.vector.quantize_mx(
-                out=codes1[:, c0:c1].bitcast(FP8X4), scales=scales1[:, c0:c1], in_=x1g[1][:, PACK * c0 : PACK * c1]
-            )
-            for i in range(c0 // P, c1 // P):
-                stage2_passes(1, i)
-                res = keep.tile([P, NP], F32, name=f"res{i}")
-                nc.vector.tensor_tensor(res[:], scores[i][:], jw_sb[:], ALU.mult)
-                nc.sync.dma_start(out[P * i : P * (i + 1), :], res[:])
+            result = keep.tile([P, NP], F32, name=f"result{i}")
+            nc.vector.tensor_tensor(result[:], scores[i][:], jw_sb[:], ALU.mult)
+            nc.sync.dma_start(out[P * i : P * (i + 1), :], result[:])

from contextlib import ExitStack

import concourse.mybir as mybir

K, H, T, S, NP = 1536, 1024, 2048, 1024, 512
FLOPS = 2 * K * H * S + 4 * H * NP * NP

F32 = mybir.dt.float32
BF16 = mybir.dt.bfloat16
I32 = mybir.dt.int32
U32 = mybir.dt.uint32
U16 = mybir.dt.uint16
U8 = mybir.dt.uint8
FP8X4 = mybir.dt.float8_e4m3fn_x4
FP4X4 = mybir.dt.float4_e2m1fn_x4
ACT = mybir.ActivationFunctionType
ALU = mybir.AluOpType

P = 128
PACK = 4
PASS = P * PACK
K_PASSES = K // PASS
R_PASSES = H // PASS
BANK = 512
QUADRANT = 32
PER_COLUMN = 16
LAST = PACK - 1
HALVES = ((0, NP // 2), (NP // 2, NP))

SCALAR_COLUMNS = {(0, 0): PASS, (1, 0): 192, (2, 0): 160, (0, 1): 0, (1, 1): PASS, (2, 1): PASS}


def tile_list_tablet_join_scores_kernel(
    tc, tab_words, tab_scales, offs, pos1, pos2, w1, w4_words, w4_scales, gain, prof, ew, jw, out
):
    nc = tc.nc
    with ExitStack() as ctx:
        keep = ctx.enter_context(tc.tile_pool(name="keep", bufs=1))
        ring = ctx.enter_context(tc.tile_pool(name="ring", bufs=3))
        psum = ctx.enter_context(tc.psum_pool(name="psum", bufs=1))

        offs_sb = keep.tile([P, S // PER_COLUMN], U16, name="offs_sb")
        pos1_sb = keep.tile([P, NP // PER_COLUMN], U16, name="pos1_sb")
        pos2_sb = keep.tile([P, NP // PER_COLUMN], U16, name="pos2_sb")
        nc.sync.dma_start(offs_sb[:], offs)

        tab_scale_sb = keep.tile([P, T], U8, name="tab_scale_sb", align_bytes=64)
        w4_scale_sb = keep.tile([P, R_PASSES, NP], U8, name="w4_scale_sb", align_bytes=64)
        nc.gpsimd.memset(tab_scale_sb[:].bitcast(I32), 0)
        nc.gpsimd.memset(w4_scale_sb[:].bitcast(I32), 0)

        tab_word_sb = []
        for a in range(K_PASSES):
            words = keep.tile([P, T], I32, name=f"tab_word_sb{a}", align_bytes=64)
            nc.sync.dma_start(words[:], tab_words[a].rearrange("p t i -> p (t i)").bitcast(I32))
            tab_word_sb.append(words)
        nc.sync.dma_start(pos2_sb[:], pos2)
        for q in range(P // QUADRANT):
            rows = slice(QUADRANT * q, QUADRANT * q + 4 * K_PASSES)
            nc.sync.dma_start(tab_scale_sb[rows, :].bitcast(I32), tab_scales[:, 4 * q : 4 * q + 4, :].bitcast(I32))

        w1_sb = {}
        for b in range(R_PASSES):
            for a in range(K_PASSES):
                w1_sb[a, b] = keep.tile([P, PACK, PASS], F32, name=f"w1_sb{a}{b}")
                piece = w1[PASS * a : PASS * (a + 1), PASS * b : PASS * (b + 1)]
                nc.sync.dma_start(w1_sb[a, b][:], piece.rearrange("(p j) c -> p j c", j=PACK))
            if b == 0:
                nc.sync.dma_start(pos1_sb[:], pos1)

        gain_sb = keep.tile([P, R_PASSES, PACK], F32, name="gain_sb")
        prof_sb = keep.tile([P, R_PASSES, PACK], F32, name="prof_sb")
        ew_sb = keep.tile([P, R_PASSES, PACK], F32, name="ew_sb")
        for dst, src in ((prof_sb, prof), (gain_sb, gain), (ew_sb, ew)):
            nc.sync.dma_start(dst[:], src.rearrange("(b p t) -> p b t", p=P, t=PACK))
        for q in range(P // QUADRANT):
            nc.sync.dma_start(
                w4_scale_sb[QUADRANT * q : QUADRANT * q + 4, :, :].bitcast(I32),
                w4_scales[:, 4 * q : 4 * q + 4, :].rearrange("b r c -> r b c").bitcast(I32),
            )
        w4_word_sb = keep.tile([P, R_PASSES, 2 * NP], U8, name="w4_word_sb", align_bytes=64)
        nc.sync.dma_start(w4_word_sb[:].bitcast(I32), w4_words.rearrange("b p c -> p b c").bitcast(I32))
        jw_sb = keep.tile([P, NP], F32, name="jw_sb")
        nc.sync.dma_start(jw_sb[:], jw.partition_broadcast(P))

        minus_prof = keep.tile([P, R_PASSES, PACK], F32, name="minus_prof")
        ew_gain = keep.tile([P, R_PASSES, PACK], F32, name="ew_gain")
        minus_ew_prof = keep.tile([P, R_PASSES, PACK], F32, name="minus_ew_prof")
        ew_sign = keep.tile([P, R_PASSES, PACK], F32, name="ew_sign")
        nc.gpsimd.tensor_scalar(minus_prof[:], prof_sb[:], -1.0, 0.0, ALU.mult, ALU.add)
        nc.gpsimd.tensor_tensor(ew_gain[:], ew_sb[:], gain_sb[:], ALU.mult)
        nc.gpsimd.tensor_tensor(minus_ew_prof[:], ew_sb[:], minus_prof[:], ALU.mult)
        nc.gpsimd.tensor_scalar(ew_sign[:], ew_sb[:], 0.0, 2.0, ALU.is_ge, ALU.mult)
        nc.gpsimd.tensor_scalar(ew_sign[:], ew_sign[:], 1.0, -1.0, ALU.mult, ALU.add)

        def mx_tiles(name):
            codes = keep.tile([P, PASS], U32, name=f"{name}_codes", align_bytes=64)
            scales = keep.tile([P, PASS], U8, name=f"{name}_scales", align_bytes=64)
            return codes, scales

        def quantise(mx, rounded, c0=0, c1=PASS):
            codes, scales = mx
            nc.vector.quantize_mx(
                out=codes[:, c0:c1].bitcast(FP8X4), scales=scales[:, c0:c1], in_=rounded[:, PACK * c0 : PACK * c1]
            )

        v_words = []
        for a in range(K_PASSES):
            picked_words = keep.tile([P, S], U32, name=f"v_words{a}", align_bytes=64)
            nc.vector.tensor_copy(picked_words[:], tab_word_sb[a][:].bitcast(U32).indirect(offs_sb[:]))
            v_words.append(picked_words)
        v_scales = keep.tile([P, S], U8, name="v_scales", align_bytes=64)
        nc.vector.tensor_copy(v_scales[:], tab_scale_sb[:].indirect(offs_sb[:]))

        w1_mx = {}

        def prepare_w1(a, b):
            rounded = ring.tile([P, PACK * PASS], BF16, name=f"w1_rounded{a}{b}", tag="w1_rounded", align_bytes=64)
            dst = rounded[:].rearrange("p (t m u e) -> p m u t e", t=PACK, u=2, e=2)
            src = w1_sb[a, b][:].rearrange("p (u e) (m t) -> p m u t e", e=2, t=PACK)
            split = SCALAR_COLUMNS[a, b] // PACK
            if split > 0:
                nc.scalar.copy(dst[:, :split], src[:, :split])
            if split < P:
                nc.vector.tensor_copy(dst[:, split:], src[:, split:])
            w1_mx[a, b] = mx_tiles(f"w1_{a}{b}")
            if (a, b) == (K_PASSES - 1, 0):
                quantise(w1_mx[a, b], rounded, 0, P)
                quantise(w1_mx[a, b], rounded, P, PASS)
            else:
                quantise(w1_mx[a, b], rounded)

        sums = {}

        def first_stage(b):
            for t in range(PACK):
                for half in range(S // BANK):
                    sums[b, t, half] = psum.tile([P, BANK], F32, name=f"sums{b}{t}{half}", tag=f"bank{2 * t + half}")
                for a in range(K_PASSES):
                    codes, scales = w1_mx[a, b]
                    for half in range(S // BANK):
                        cols = slice(BANK * half, BANK * (half + 1))
                        nc.tensor.matmul_mx(
                            out=sums[b, t, half][:],
                            lhsT=codes[:, P * t : P * (t + 1)].bitcast(FP8X4),
                            lhsT_scale=scales[:, P * t : P * (t + 1)],
                            rhs=v_words[a][:, cols].bitcast(FP8X4),
                            rhs_scale=v_scales[4 * a :, cols],
                            start=(a == 0),
                            stop=(a == K_PASSES - 1),
                        )

        upper = [keep.tile([P, PACK, NP], F32, name=f"upper{b}") for b in range(R_PASSES)]
        lower = [keep.tile([P, PACK, NP], F32, name=f"lower{b}") for b in range(R_PASSES)]
        x1_rows = [keep.tile([P, PACK, NP], BF16, name=f"x1_rows{b}") for b in range(R_PASSES)]
        x2_rows = [keep.tile([P, PACK, NP], BF16, name=f"x2_rows{b}") for b in range(R_PASSES)]
        x1_woven = [keep.tile([P, PACK * NP], BF16, name=f"x1_woven{b}", align_bytes=64) for b in range(R_PASSES)]
        x2_woven = [keep.tile([P, PACK * NP], BF16, name=f"x2_woven{b}", align_bytes=64) for b in range(R_PASSES)]
        x1_mx = [mx_tiles(f"x1_{b}") for b in range(R_PASSES)]
        x2_mx = [mx_tiles(f"x2_{b}") for b in range(R_PASSES)]
        tanh_sb = {}

        def tanh_slice(b, t):
            tanh_sb[b, t] = keep.tile([P, S], F32, name=f"tanh_sb{b}{t}")
            for half in range(S // BANK):
                nc.scalar.activation(tanh_sb[b, t][:, BANK * half : BANK * (half + 1)], sums[b, t, half][:], ACT.Tanh)

        def pick(dst, pos_sb, b, t, c0=0, c1=NP):
            offsets = pos_sb[:, c0 // PER_COLUMN : c1 // PER_COLUMN]
            nc.vector.tensor_copy(dst[b][:, t, c0:c1], tanh_sb[b, t][:].indirect(offsets))

        def tanh_and_pick(b, t):
            tanh_slice(b, t)
            pick(lower, pos2_sb, b, t)
            pick(upper, pos1_sb, b, t)

        def make_x1(b, t):
            nc.scalar.activation(
                x1_rows[b][:, t, :],
                upper[b][:, t, :],
                ACT.Identity,
                bias=minus_prof[:, b, t : t + 1],
                scale=gain_sb[:, b, t : t + 1],
            )

        def make_x2(b, t, c0=0, c1=NP):
            x2 = x2_rows[b][:, t, c0:c1]
            nc.scalar.activation(
                x2, lower[b][:, t, c0:c1], ACT.Abs, bias=minus_ew_prof[:, b, t : t + 1], scale=ew_gain[:, b, t : t + 1]
            )
            nc.vector.tensor_scalar(x2, x2, ew_sign[:, b, t : t + 1], None, ALU.mult)

        def weave(copy, woven, rows, c0=0, c1=NP):
            copy(
                woven[:, PACK * c0 : PACK * c1].rearrange("p (c t) -> p c t", t=PACK),
                rows[:, :, c0:c1].rearrange("p t c -> p c t"),
            )

        for a in range(K_PASSES):
            prepare_w1(a, 0)
        first_stage(0)
        prepare_w1(0, 1)
        tanh_and_pick(0, 0)
        for t in range(1, LAST):
            tanh_and_pick(0, t)
            prepare_w1(t, 1)
        tanh_and_pick(0, LAST)

        first_stage(1)
        for t in range(LAST):
            make_x2(0, t)
        tanh_and_pick(1, 0)
        make_x2(0, LAST)
        make_x1(0, 0)
        weave(nc.vector.tensor_copy, x2_woven[0], x2_rows[0])
        quantise(x2_mx[0], x2_woven[0])
        tanh_and_pick(1, 1)
        for t in range(1, PACK):
            make_x1(0, t)
        tanh_and_pick(1, 2)
        tanh_slice(1, LAST)
        pick(upper, pos1_sb, 1, LAST)
        for c0, c1 in HALVES:
            pick(lower, pos2_sb, 1, LAST, c0, c1)
        weave(nc.scalar.copy, x1_woven[0], x1_rows[0])
        quantise(x1_mx[0], x1_woven[0])

        scores = [psum.tile([P, NP], F32, name=f"scores{i}", tag=f"bank{i}") for i in range(NP // P)]

        def second_stage(b):
            codes, scales = x1_mx[b]
            w4_operand = (w4_word_sb[:, b, :].bitcast(FP4X4), w4_scale_sb[:, b, :])
            x2_operand = (x2_mx[b][0][:].bitcast(FP8X4), x2_mx[b][1][:])
            for i in range(NP // P):
                rows = slice(P * i, P * (i + 1))
                for n, (rhs, rhs_scale) in enumerate((w4_operand, x2_operand)):
                    nc.tensor.matmul_mx(
                        out=scores[i][:],
                        lhsT=codes[:, rows].bitcast(FP8X4),
                        lhsT_scale=scales[:, rows],
                        rhs=rhs,
                        rhs_scale=rhs_scale,
                        start=(b == 0 and n == 0),
                        stop=(b == R_PASSES - 1 and n == 1),
                    )

        second_stage(0)
        for t in range(LAST):
            make_x2(1, t)
        for t in range(LAST):
            make_x1(1, t)
        for c0, c1 in HALVES:
            make_x2(1, LAST, c0, c1)
            weave(nc.vector.tensor_copy, x2_woven[1], x2_rows[1], c0, c1)
        quantise(x2_mx[1], x2_woven[1])
        make_x1(1, LAST)
        for c0, c1 in HALVES:
            weave(nc.scalar.copy, x1_woven[1], x1_rows[1], c0, c1)
            quantise(x1_mx[1], x1_woven[1], c0, c1)
        second_stage(1)

        for i in range(NP // P):
            result = keep.tile([P, NP], F32, name=f"result{i}")
            nc.vector.tensor_tensor(result[:], scores[i][:], jw_sb[:], ALU.mult)
            nc.sync.dma_start(out[P * i : P * (i + 1), :], result[:])
